import numpy as np
import ml_dtypes


def mxq(x, axis, fmt="e4m3"):
    dtype, down = {"e4m3": (ml_dtypes.float8_e4m3fn, 7), "e5m2": (ml_dtypes.float8_e5m2, 14)}[fmt]
    v = np.moveaxis(np.asarray(x, np.float32).astype(ml_dtypes.bfloat16).astype(np.float64), axis, -1)
    blocks = v.reshape(v.shape[:-1] + (-1, 32))
    amax = np.abs(blocks).max(-1, keepdims=True)
    byte = np.maximum(np.where(amax > 0, np.frexp(amax)[1] - 1 + 127, 0) - down, 1)
    scale = np.exp2(byte - 127.0)
    codes = (blocks / scale).astype(np.float32).astype(dtype).astype(np.float64)
    return np.moveaxis((codes * scale).reshape(v.shape), -1, axis)


WIDE = False


def mx_kscale(k):
    if not WIDE:
        return np.ones(k)
    levels = np.array([10, -10, 5, -5, 0])
    if k % 512:
        return np.exp2(np.random.permutation(np.resize(levels, k // 32))).repeat(32)
    a = np.empty((k // 512, 16))
    for p in range(k // 512):
        a[p, :8] = np.random.permutation(np.resize(levels, 8))
        for g in range(8):
            far = levels[np.abs(levels - a[p, g]) >= 10]
            a[p, g + 8] = far[np.random.randint(len(far))]
    return np.exp2(a.ravel()).repeat(32)


def f64(x):
    return np.asarray(x).astype(np.float64)


def striped(idx):
    return np.tile(idx.reshape(-1, 16).T, (8, 1)).astype(np.uint16)


def unstriped(offs):
    return offs[:16].T.reshape(-1).astype(np.int64)


E2M1 = np.array([0.0, 0.5, 1.0, 1.5, 2.0, 3.0, 4.0, 6.0, -0.0, -0.5, -1.0, -1.5, -2.0, -3.0, -4.0, -6.0])


def pack_weight(w, fmt):
    k, n = w.shape
    w = f64(np.asarray(w, np.float32).astype(ml_dtypes.bfloat16)).reshape(k // 32, 32, n)
    amax = np.abs(w).max(1)
    if fmt == "e4m3":
        byte = np.frexp(amax)[1] - 1 + 127 - 7
    else:
        mant, ex = np.frexp(amax / 6.0)
        byte = np.where(mant > 0.5, ex, ex - 1) + 127
    byte = np.clip(np.where(amax > 0, byte, 1), 1, 254)
    scaled = (w * np.exp2(127.0 - byte)[:, None, :]).reshape(k, n).astype(np.float32)
    by_word = np.ascontiguousarray(scaled.reshape(k // 512, 128, 4, n).transpose(0, 1, 3, 2))
    if fmt == "e4m3":
        words = by_word.astype(ml_dtypes.float8_e4m3fn).view(np.uint8)
    else:
        c = by_word.astype(ml_dtypes.float4_e2m1fn).view(np.uint8) & 0xF
        words = (c[..., 0::2] | (c[..., 1::2] << 4)).reshape(k // 512, 128, 2 * n)
    return np.ascontiguousarray(words), np.ascontiguousarray(byte.astype(np.uint8).reshape(k // 512, 16, n))


def unpack_weight(words, scales, fmt):
    g, _, n = scales.shape
    words = np.ascontiguousarray(words).reshape(g, 128, n, -1)
    if fmt == "e4m3":
        vals = words.view(ml_dtypes.float8_e4m3fn).astype(np.float64)
    else:
        nib = np.empty((g, 128, n, 4), np.uint8)
        nib[..., 0::2] = words & 0xF
        nib[..., 1::2] = words >> 4
        vals = E2M1[nib]
    vals = vals * np.repeat(np.exp2(scales.astype(np.float64) - 127.0), 8, axis=1)[..., None]
    return vals.transpose(0, 1, 3, 2).reshape(g * 512, n)


def gelu(v):
    return 0.5 * v * (1.0 + np.tanh(np.sqrt(2.0 / np.pi) * (v + 0.044715 * v**3)))


K, T, E, C, N = 1024, 1024, 4, 256, 256
R = 2


def by_expert(wq, xq):
    return np.concatenate([wq[e].T @ xq[:, e * C:(e + 1) * C] for e in range(E)], axis=1)


def setup_inputs():
    n = np.random.standard_normal
    s = mx_kscale(K)[:, None]
    slot_token = np.concatenate([r * (T // R) + np.random.permutation(T // R)[:C // R] for e in range(E) for r in range(R)])
    w = [pack_weight(m, "e2m1") for m in n((E, K, N)) / np.sqrt(K) / s[None]]
    return {
        "xT": (n((K, T)) * s).astype(np.float32),
        "w_words": np.stack([m[0] for m in w]),
        "w_scales": np.stack([m[1] for m in w]),
        "b": (0.3 * n((N, E))).astype(np.float32),
        "offs": striped(slot_token),
    }


def reference(xT, w_words, w_scales, b, offs):
    idx = unstriped(offs)
    w = np.stack([unpack_weight(w_words[e], w_scales[e], "e2m1") for e in range(E)])
    xq = mxq(f64(xT)[:, idx], 0, "e4m3")
    y = by_expert(w, xq)
    y = gelu(y + np.repeat(f64(b), C, axis=1))
    return y.reshape(N, E, R, C // R).transpose(0, 2, 1, 3).reshape(N, E * C)

@@ -1,0 +1,179 @@
+from contextlib import ExitStack
+
+import concourse.mybir as mybir
+
+K, T, E, N = 1024, 1024, 4, 256
+RANKS = 2
+P = 128
+PACK = 4
+PASSES = K // (P * PACK)
+RT = T // RANKS
+SLOTS = 128
+CHUNK = 256
+HALVES = N // P
+
+FLOPS = 2 * K * N * T
+BYTES = 4 * K * T + E * K * N // 2 + E * K * N // 32 + 4 * N * E + 2 * P * T // 16 + 4 * N * T
+
+F32 = mybir.dt.float32
+BF16 = mybir.dt.bfloat16
+I32 = mybir.dt.int32
+U32 = mybir.dt.uint32
+U16 = mybir.dt.uint16
+U8 = mybir.dt.uint8
+FP8X4 = mybir.dt.float8_e4m3fn_x4
+FP4X4 = mybir.dt.float4_e2m1fn_x4
+ACT = mybir.ActivationFunctionType
+
+
+def tile_moe_eps_lin_gelu_kernel(tc, xT, w_words, w_scales, b, offs, out):
+    nc = tc.nc
+    with ExitStack() as ctx:
+        keep = ctx.enter_context(tc.tile_pool(name="keep", bufs=1))
+        psum = ctx.enter_context(tc.psum_pool(name="psum", bufs=1))
+
+        offsets = keep.tile([P, T // 16], U16, name="offsets")
+        warm = keep.tile([P, 8], F32, name="warm")
+        warm_out = keep.tile([P, 8], F32, name="warm_out")
+        bias = keep.tile([P, HALVES, E], F32, name="bias")
+        codes_w = keep.tile([P, E * PASSES, 2 * N], U8, name="codes_w", align_bytes=64)
+        scales_w = keep.tile([P, E * PASSES, N], U8, name="scales_w", align_bytes=64)
+        words = [keep.tile([P, T], U32, name=f"words{a}", align_bytes=64) for a in range(PASSES)]
+        scales = keep.tile([P, T], U8, name="scales", align_bytes=64)
+        g_words = [keep.tile([P, T], U32, name=f"g_words{a}", align_bytes=64) for a in range(PASSES)]
+        g_scales = keep.tile([P, T], U8, name="g_scales", align_bytes=64)
+        shifted = keep.tile([P, T], U8, name="shifted", align_bytes=64)
+
+        nc.vector.memset(warm[:], 0.0)
+        nc.scalar.activation(warm_out[:], warm[:], ACT.Gelu_apprx_tanh)
+        nc.vector.memset(scales[:].bitcast(I32), 0)
+        nc.vector.memset(shifted[:].bitcast(I32), 0)
+        nc.vector.memset(scales_w[:].rearrange("p g n -> p (g n)").bitcast(I32), 0)
+
+        order = [(m, a, c) for m in range(RANKS) for a in range(PASSES) for c in range(RT // CHUNK)]
+        raw = {}
+
+        def load(i):
+            m, a, c = order[i]
+            t0 = m * RT + c * CHUNK
+            tile = keep.tile([P, PACK, CHUNK], F32, name=f"raw{i}")
+            nc.sync.dma_start(
+                out=tile[:],
+                in_=xT[512 * a:512 * (a + 1), t0:t0 + CHUNK].rearrange("(p t) w -> p t w", t=PACK),
+            )
+            raw[i] = tile
+
+        load(0)
+        load(1)
+        nc.sync.dma_start(offsets[:], offs)
+        for i in range(2, 8):
+            load(i)
+        nc.sync.dma_start(
+            out=codes_w[:].rearrange("p g n -> p (g n)").bitcast(I32).rearrange("p (g n) -> p g n", g=E * PASSES),
+            in_=w_words.bitcast(I32).rearrange("e a p n -> p (e a) n"),
+        )
+        for q in range(4):
+            nc.sync.dma_start(
+                out=scales_w[32 * q:32 * q + 4].rearrange("p g n -> p (g n)").bitcast(I32).rearrange("p (g n) -> p g n", g=E * PASSES),
+                in_=w_scales.bitcast(I32).rearrange("e a q n -> q (e a) n")[4 * q:4 * q + 4],
+            )
+        nc.sync.dma_start(out=bias[:], in_=b.rearrange("(h p) e -> p h e", p=P))
+
+        v_share = [160, 160, 0, 0, 0, 0, 0, 0]
+        grouped = {}
+
+        def interleave(i):
+            tile = keep.tile([P, CHUNK * PACK], BF16, name=f"grouped{i}", align_bytes=64)
+            grouped[i] = tile
+            dst = tile[:].rearrange("p (c i t) -> p c t i", i=4, t=PACK)
+            src = raw[i][:].rearrange("p t (c i) -> p c t i", i=4)
+            v = v_share[i] // 4
+            if v:
+                nc.vector.tensor_copy(dst[:, :v], src[:, :v])
+            if v < CHUNK // 4:
+                nc.scalar.activation(dst[:, v:], src[:, v:], ACT.Copy)
+
+        def quantize(i):
+            m, a, c = order[i]
+            t0 = m * RT + c * CHUNK
+            nc.vector.quantize_mx(
+                out=words[a][:, t0:t0 + CHUNK].bitcast(FP8X4), scales=scales[4 * a:, t0:t0 + CHUNK], in_=grouped[i][:]
+            )
+
+        def gather(m, e, src, dst):
+            window = src[:, 0:RT] if m == 0 else src[:]
+            col = 16 * e + 8 * m
+            o0 = RT * m + SLOTS * e
+            nc.vector.tensor_copy(dst[:, o0:o0 + SLOTS], window.indirect(offsets[:, col:col + 8]))
+
+        banks = {}
+        results = {}
+
+        def multiply(m, e):
+            acc = psum.tile([P, HALVES, SLOTS], F32, name=f"acc{m}{e}")
+            banks[m, e] = acc
+            o0 = RT * m + SLOTS * e
+            for h in range(HALVES):
+                for a in range(PASSES):
+                    g = e * PASSES + a
+                    nc.tensor.matmul_mx(
+                        out=acc[:, h, :],
+                        lhsT=codes_w[:, g, 2 * P * h:2 * P * (h + 1)].bitcast(FP4X4),
+                        lhsT_scale=scales_w[:, g, P * h:P * (h + 1)],
+                        rhs=g_words[a][:, o0:o0 + SLOTS].bitcast(FP8X4),
+                        rhs_scale=(shifted if a else g_scales)[:, o0:o0 + SLOTS],
+                        start=(a == 0),
+                        stop=(a == PASSES - 1),
+                    )
+
+        def finish(m, e):
+            for h in range(HALVES):
+                if e == 0:
+                    results[m, h] = keep.tile([P, RT], F32, name=f"result{m}{h}")
+                nc.scalar.activation(
+                    results[m, h][:, SLOTS * e:SLOTS * (e + 1)], banks[m, e][:, h, :], ACT.Gelu_apprx_tanh, bias=bias[:, h, e:e + 1]
+                )
+                if e % 2 == 1:
+                    c0 = SLOTS * (e - 1)
+                    (nc.scalar if m == 0 else nc.sync).dma_start(
+                        out=out[P * h:P * (h + 1), RT * m + c0:RT * m + c0 + 2 * SLOTS], in_=results[m, h][:, c0:c0 + 2 * SLOTS]
+                    )
+
+        def shift(m):
+            cols = slice(RT * m, RT * (m + 1))
+            for q in range(4):
+                nc.sync.dma_start(
+                    out=shifted[32 * q:32 * q + 4, cols].bitcast(I32), in_=g_scales[32 * q + 4:32 * q + 8, cols].bitcast(I32)
+                )
+
+        for i in range(8):
+            interleave(i)
+
+        quantize(0)
+        quantize(1)
+        for e in range(E):
+            gather(0, e, words[0], g_words[0])
+        quantize(2)
+        quantize(3)
+        for e in range(E):
+            gather(0, e, scales, g_scales)
+        shift(0)
+        for e in range(E):
+            gather(0, e, words[1], g_words[1])
+        quantize(4)
+        quantize(5)
+        gather(1, 0, words[0], g_words[0])
+        gather(1, 1, words[0], g_words[0])
+        quantize(6)
+        quantize(7)
+        for e in range(E):
+            gather(1, e, scales, g_scales)
+        shift(1)
+        gather(1, 2, words[0], g_words[0])
+        gather(1, 3, words[0], g_words[0])
+        for e in range(E):
+            gather(1, e, words[1], g_words[1])
+        for m in range(RANKS):
+            for e in range(E):
+                multiply(m, e)
+                finish(m, e)

@@ -9,7 +9,6 @@ PACK = 4
 PASSES = K // (P * PACK)
 RT = T // RANKS
 SLOTS = 128
-CHUNK = 256
 HALVES = N // P
 
 FLOPS = 2 * K * N * T
@@ -24,6 +23,15 @@ U8 = mybir.dt.uint8
 FP8X4 = mybir.dt.float8_e4m3fn_x4
 FP4X4 = mybir.dt.float4_e2m1fn_x4
 ACT = mybir.ActivationFunctionType
+
+CHUNKS = [
+    (0, 0, 0, 256, 160),
+    (0, 0, 256, 256, 160),
+    (0, 1, 0, 512, 304),
+    (1, 0, 512, 512, 0),
+    (1, 1, 512, 512, 128),
+]
+ROW = {0: 4, 1: 0}
 
 
 def tile_moe_eps_lin_gelu_kernel(tc, xT, w_words, w_scales, b, offs, out):
@@ -42,6 +50,7 @@ def tile_moe_eps_lin_gelu_kernel(tc, xT, w_words, w_scales, b, offs, out):
         scales = keep.tile([P, T], U8, name="scales", align_bytes=64)
         g_words = [keep.tile([P, T], U32, name=f"g_words{a}", align_bytes=64) for a in range(PASSES)]
         g_scales = keep.tile([P, T], U8, name="g_scales", align_bytes=64)
+        g_early = keep.tile([P, 2 * SLOTS], U8, name="g_early", align_bytes=64)
         shifted = keep.tile([P, T], U8, name="shifted", align_bytes=64)
 
         nc.vector.memset(warm[:], 0.0)
@@ -50,24 +59,15 @@ def tile_moe_eps_lin_gelu_kernel(tc, xT, w_words, w_scales, b, offs, out):
         nc.vector.memset(shifted[:].bitcast(I32), 0)
         nc.vector.memset(scales_w[:].rearrange("p g n -> p (g n)").bitcast(I32), 0)
 
-        order = [(m, a, c) for m in range(RANKS) for a in range(PASSES) for c in range(RT // CHUNK)]
-        raw = {}
-
-        def load(i):
-            m, a, c = order[i]
-            t0 = m * RT + c * CHUNK
-            tile = keep.tile([P, PACK, CHUNK], F32, name=f"raw{i}")
+        raw = []
+        for i, (m, a, t0, width, v) in enumerate(CHUNKS):
+            tile = keep.tile([P, PACK, width], F32, name=f"raw{i}")
             nc.sync.dma_start(
-                out=tile[:],
-                in_=xT[512 * a:512 * (a + 1), t0:t0 + CHUNK].rearrange("(p t) w -> p t w", t=PACK),
+                out=tile[:], in_=xT[512 * a:512 * (a + 1), t0:t0 + width].rearrange("(p t) w -> p t w", t=PACK)
             )
-            raw[i] = tile
-
-        load(0)
-        load(1)
-        nc.sync.dma_start(offsets[:], offs)
-        for i in range(2, 8):
-            load(i)
+            raw.append(tile)
+            if i == 1:
+                nc.sync.dma_start(offsets[:], offs)
         nc.sync.dma_start(
             out=codes_w[:].rearrange("p g n -> p (g n)").bitcast(I32).rearrange("p (g n) -> p g n", g=E * PASSES),
             in_=w_words.bitcast(I32).rearrange("e a p n -> p (e a) n"),
@@ -79,40 +79,56 @@ def tile_moe_eps_lin_gelu_kernel(tc, xT, w_words, w_scales, b, offs, out):
             )
         nc.sync.dma_start(out=bias[:], in_=b.rearrange("(h p) e -> p h e", p=P))
 
-        v_share = [160, 160, 0, 0, 0, 0, 0, 0]
-        grouped = {}
+        grouped = []
 
         def interleave(i):
-            tile = keep.tile([P, CHUNK * PACK], BF16, name=f"grouped{i}", align_bytes=64)
-            grouped[i] = tile
+            m, a, t0, width, v = CHUNKS[i]
+            tile = keep.tile([P, width * PACK], BF16, name=f"grouped{i}", align_bytes=64)
+            grouped.append(tile)
             dst = tile[:].rearrange("p (c i t) -> p c t i", i=4, t=PACK)
             src = raw[i][:].rearrange("p t (c i) -> p c t i", i=4)
-            v = v_share[i] // 4
+            end = (width - v) // 4
+            for s in range(0, end, 64):
+                e = min(s + 64, end)
+                nc.scalar.activation(dst[:, s:e], src[:, s:e], ACT.Copy)
             if v:
-                nc.vector.tensor_copy(dst[:, :v], src[:, :v])
-            if v < CHUNK // 4:
-                nc.scalar.activation(dst[:, v:], src[:, v:], ACT.Copy)
+                nc.vector.tensor_copy(dst[:, end:], src[:, end:])
 
-        def quantize(i):
-            m, a, c = order[i]
-            t0 = m * RT + c * CHUNK
+        def quantize(i, half=None):
+            m, a, t0, width, v = CHUNKS[i]
+            t1 = t0 + half * width // 2 if half else t0
+            n = width if half is None else width // 2
+            o = t1 - t0
             nc.vector.quantize_mx(
-                out=words[a][:, t0:t0 + CHUNK].bitcast(FP8X4), scales=scales[4 * a:, t0:t0 + CHUNK], in_=grouped[i][:]
+                out=words[a][:, t1:t1 + n].bitcast(FP8X4), scales=scales[ROW[a]:, t1:t1 + n], in_=grouped[i][:, PACK * o:PACK * (o + n)]
             )
 
         def gather(m, e, src, dst):
             window = src[:, 0:RT] if m == 0 else src[:]
             col = 16 * e + 8 * m
-            o0 = RT * m + SLOTS * e
-            nc.vector.tensor_copy(dst[:, o0:o0 + SLOTS], window.indirect(offsets[:, col:col + 8]))
+            nc.vector.tensor_copy(dst, window.indirect(offsets[:, col:col + 8]))
+
+        def slots(m, e, count=1):
+            return slice(RT * m + SLOTS * e, RT * m + SLOTS * (e + count))
+
+        def gather_words(m, a, e):
+            gather(m, e, words[a], g_words[a][:, slots(m, e)])
+
+        def gather_scales(m, e):
+            gather(m, e, scales, g_scales[:, slots(m, e)])
+
+        def shift(cols, src):
+            for q in range(4):
+                nc.sync.dma_start(
+                    out=shifted[32 * q:32 * q + 4, cols].bitcast(I32), in_=src[32 * q + 4:32 * q + 8].bitcast(I32)
+                )
 
         banks = {}
-        results = {}
+        results = {(m, h): keep.tile([P, RT], F32, name=f"result{m}{h}") for m in range(RANKS) for h in range(HALVES)}
 
         def multiply(m, e):
             acc = psum.tile([P, HALVES, SLOTS], F32, name=f"acc{m}{e}")
             banks[m, e] = acc
-            o0 = RT * m + SLOTS * e
             for h in range(HALVES):
                 for a in range(PASSES):
                     g = e * PASSES + a
@@ -120,60 +136,67 @@ def tile_moe_eps_lin_gelu_kernel(tc, xT, w_words, w_scales, b, offs, out):
                         out=acc[:, h, :],
                         lhsT=codes_w[:, g, 2 * P * h:2 * P * (h + 1)].bitcast(FP4X4),
                         lhsT_scale=scales_w[:, g, P * h:P * (h + 1)],
-                        rhs=g_words[a][:, o0:o0 + SLOTS].bitcast(FP8X4),
-                        rhs_scale=(shifted if a else g_scales)[:, o0:o0 + SLOTS],
+                        rhs=g_words[a][:, slots(m, e)].bitcast(FP8X4),
+                        rhs_scale=(g_scales if a else shifted)[:, slots(m, e)],
                         start=(a == 0),
                         stop=(a == PASSES - 1),
                     )
 
-        def finish(m, e):
+        def activate(m, e):
             for h in range(HALVES):
-                if e == 0:
-                    results[m, h] = keep.tile([P, RT], F32, name=f"result{m}{h}")
                 nc.scalar.activation(
                     results[m, h][:, SLOTS * e:SLOTS * (e + 1)], banks[m, e][:, h, :], ACT.Gelu_apprx_tanh, bias=bias[:, h, e:e + 1]
                 )
-                if e % 2 == 1:
-                    c0 = SLOTS * (e - 1)
-                    (nc.scalar if m == 0 else nc.sync).dma_start(
-                        out=out[P * h:P * (h + 1), RT * m + c0:RT * m + c0 + 2 * SLOTS], in_=results[m, h][:, c0:c0 + 2 * SLOTS]
-                    )
 
-        def shift(m):
-            cols = slice(RT * m, RT * (m + 1))
-            for q in range(4):
-                nc.sync.dma_start(
-                    out=shifted[32 * q:32 * q + 4, cols].bitcast(I32), in_=g_scales[32 * q + 4:32 * q + 8, cols].bitcast(I32)
+        def store(m, e, count, queues):
+            for h in range(HALVES):
+                queues[h].dma_start(
+                    out=out[P * h:P * (h + 1), slots(m, e, count)], in_=results[m, h][:, SLOTS * e:SLOTS * (e + count)]
                 )
 
-        for i in range(8):
+        for i in range(len(CHUNKS)):
             interleave(i)
 
         quantize(0)
         quantize(1)
         for e in range(E):
-            gather(0, e, words[0], g_words[0])
+            gather_words(0, 0, e)
         quantize(2)
+        for e in range(E):
+            gather_scales(0, e)
+        shift(slots(0, 0, E), g_scales[:, slots(0, 0, E)])
+        for e in range(E):
+            gather_words(0, 1, e)
         quantize(3)
+        for j, e in enumerate((2, 3)):
+            gather(1, e, scales, g_early[:, SLOTS * j:SLOTS * (j + 1)])
+        shift(slots(1, 2, 2), g_early[:])
+        gather_words(1, 0, 2)
+        quantize(4, 0)
+        quantize(4, 1)
+        gather_scales(1, 0)
+        gather_scales(1, 1)
+        shift(slots(1, 0, 2), g_scales[:, slots(1, 0, 2)])
+        gather_scales(1, 2)
+        gather_words(1, 1, 2)
+        gather_words(1, 0, 3)
+        gather_scales(1, 3)
+        gather_words(1, 1, 3)
+        gather_words(1, 0, 0)
+        gather_words(1, 0, 1)
+        gather_words(1, 1, 0)
+        gather_words(1, 1, 1)
+
         for e in range(E):
-            gather(0, e, scales, g_scales)
-        shift(0)
+            multiply(0, e)
         for e in range(E):
-            gather(0, e, words[1], g_words[1])
-        quantize(4)
-        quantize(5)
-        gather(1, 0, words[0], g_words[0])
-        gather(1, 1, words[0], g_words[0])
-        quantize(6)
-        quantize(7)
-        for e in range(E):
-            gather(1, e, scales, g_scales)
-        shift(1)
-        gather(1, 2, words[0], g_words[0])
-        gather(1, 3, words[0], g_words[0])
-        for e in range(E):
-            gather(1, e, words[1], g_words[1])
-        for m in range(RANKS):
-            for e in range(E):
-                multiply(m, e)
-                finish(m, e)
+            activate(0, e)
+            if e % 2 == 1:
+                store(0, e - 1, 2, (nc.scalar, nc.scalar))
+        for e in (2, 3, 0, 1):
+            multiply(1, e)
+            activate(1, e)
+            if e == 3:
+                store(1, 2, 2, (nc.sync, nc.sync))
+            if e < 2:
+                store(1, e, 1, (nc.sync, nc.scalar))

from contextlib import ExitStack

import concourse.mybir as mybir

K, T, E, N = 1024, 1024, 4, 256
RANKS = 2
P = 128
PACK = 4
PASSES = K // (P * PACK)
RT = T // RANKS
SLOTS = 128
HALVES = N // P

FLOPS = 2 * K * N * T
BYTES = 4 * K * T + E * K * N // 2 + E * K * N // 32 + 4 * N * E + 2 * P * T // 16 + 4 * N * T

F32 = mybir.dt.float32
BF16 = mybir.dt.bfloat16
I32 = mybir.dt.int32
U32 = mybir.dt.uint32
U16 = mybir.dt.uint16
U8 = mybir.dt.uint8
FP8X4 = mybir.dt.float8_e4m3fn_x4
FP4X4 = mybir.dt.float4_e2m1fn_x4
ACT = mybir.ActivationFunctionType

CHUNKS = [
    (0, 0, 0, 256, 160),
    (0, 0, 256, 256, 160),
    (0, 1, 0, 512, 304),
    (1, 0, 512, 512, 0),
    (1, 1, 512, 512, 128),
]
ROW = {0: 4, 1: 0}


def tile_moe_eps_lin_gelu_kernel(tc, xT, w_words, w_scales, b, offs, out):
    nc = tc.nc
    with ExitStack() as ctx:
        keep = ctx.enter_context(tc.tile_pool(name="keep", bufs=1))
        psum = ctx.enter_context(tc.psum_pool(name="psum", bufs=1))

        offsets = keep.tile([P, T // 16], U16, name="offsets")
        warm = keep.tile([P, 8], F32, name="warm")
        warm_out = keep.tile([P, 8], F32, name="warm_out")
        bias = keep.tile([P, HALVES, E], F32, name="bias")
        codes_w = keep.tile([P, E * PASSES, 2 * N], U8, name="codes_w", align_bytes=64)
        scales_w = keep.tile([P, E * PASSES, N], U8, name="scales_w", align_bytes=64)
        words = [keep.tile([P, T], U32, name=f"words{a}", align_bytes=64) for a in range(PASSES)]
        scales = keep.tile([P, T], U8, name="scales", align_bytes=64)
        g_words = [keep.tile([P, T], U32, name=f"g_words{a}", align_bytes=64) for a in range(PASSES)]
        g_scales = keep.tile([P, T], U8, name="g_scales", align_bytes=64)
        g_early = keep.tile([P, 2 * SLOTS], U8, name="g_early", align_bytes=64)
        shifted = keep.tile([P, T], U8, name="shifted", align_bytes=64)

        nc.vector.memset(warm[:], 0.0)
        nc.scalar.activation(warm_out[:], warm[:], ACT.Gelu_apprx_tanh)
        nc.vector.memset(scales[:].bitcast(I32), 0)
        nc.vector.memset(shifted[:].bitcast(I32), 0)
        nc.vector.memset(scales_w[:].rearrange("p g n -> p (g n)").bitcast(I32), 0)

        raw = []
        for i, (m, a, t0, width, v) in enumerate(CHUNKS):
            tile = keep.tile([P, PACK, width], F32, name=f"raw{i}")
            nc.sync.dma_start(
                out=tile[:], in_=xT[512 * a:512 * (a + 1), t0:t0 + width].rearrange("(p t) w -> p t w", t=PACK)
            )
            raw.append(tile)
            if i == 1:
                nc.sync.dma_start(offsets[:], offs)
        nc.sync.dma_start(
            out=codes_w[:].rearrange("p g n -> p (g n)").bitcast(I32).rearrange("p (g n) -> p g n", g=E * PASSES),
            in_=w_words.bitcast(I32).rearrange("e a p n -> p (e a) n"),
        )
        for q in range(4):
            nc.sync.dma_start(
                out=scales_w[32 * q:32 * q + 4].rearrange("p g n -> p (g n)").bitcast(I32).rearrange("p (g n) -> p g n", g=E * PASSES),
                in_=w_scales.bitcast(I32).rearrange("e a q n -> q (e a) n")[4 * q:4 * q + 4],
            )
        nc.sync.dma_start(out=bias[:], in_=b.rearrange("(h p) e -> p h e", p=P))

        grouped = []

        def interleave(i):
            m, a, t0, width, v = CHUNKS[i]
            tile = keep.tile([P, width * PACK], BF16, name=f"grouped{i}", align_bytes=64)
            grouped.append(tile)
            dst = tile[:].rearrange("p (c i t) -> p c t i", i=4, t=PACK)
            src = raw[i][:].rearrange("p t (c i) -> p c t i", i=4)
            end = (width - v) // 4
            for s in range(0, end, 64):
                e = min(s + 64, end)
                nc.scalar.activation(dst[:, s:e], src[:, s:e], ACT.Copy)
            if v:
                nc.vector.tensor_copy(dst[:, end:], src[:, end:])

        def quantize(i, half=None):
            m, a, t0, width, v = CHUNKS[i]
            t1 = t0 + half * width // 2 if half else t0
            n = width if half is None else width // 2
            o = t1 - t0
            nc.vector.quantize_mx(
                out=words[a][:, t1:t1 + n].bitcast(FP8X4), scales=scales[ROW[a]:, t1:t1 + n], in_=grouped[i][:, PACK * o:PACK * (o + n)]
            )

        def gather(m, e, src, dst):
            window = src[:, 0:RT] if m == 0 else src[:]
            col = 16 * e + 8 * m
            nc.vector.tensor_copy(dst, window.indirect(offsets[:, col:col + 8]))

        def slots(m, e, count=1):
            return slice(RT * m + SLOTS * e, RT * m + SLOTS * (e + count))

        def gather_words(m, a, e):
            gather(m, e, words[a], g_words[a][:, slots(m, e)])

        def gather_scales(m, e):
            gather(m, e, scales, g_scales[:, slots(m, e)])

        def shift(cols, src):
            for q in range(4):
                nc.sync.dma_start(
                    out=shifted[32 * q:32 * q + 4, cols].bitcast(I32), in_=src[32 * q + 4:32 * q + 8].bitcast(I32)
                )

        banks = {}
        results = {(m, h): keep.tile([P, RT], F32, name=f"result{m}{h}") for m in range(RANKS) for h in range(HALVES)}

        def multiply(m, e):
            acc = psum.tile([P, HALVES, SLOTS], F32, name=f"acc{m}{e}")
            banks[m, e] = acc
            for h in range(HALVES):
                for a in range(PASSES):
                    g = e * PASSES + a
                    nc.tensor.matmul_mx(
                        out=acc[:, h, :],
                        lhsT=codes_w[:, g, 2 * P * h:2 * P * (h + 1)].bitcast(FP4X4),
                        lhsT_scale=scales_w[:, g, P * h:P * (h + 1)],
                        rhs=g_words[a][:, slots(m, e)].bitcast(FP8X4),
                        rhs_scale=(g_scales if a else shifted)[:, slots(m, e)],
                        start=(a == 0),
                        stop=(a == PASSES - 1),
                    )

        def activate(m, e):
            for h in range(HALVES):
                nc.scalar.activation(
                    results[m, h][:, SLOTS * e:SLOTS * (e + 1)], banks[m, e][:, h, :], ACT.Gelu_apprx_tanh, bias=bias[:, h, e:e + 1]
                )

        def store(m, e, count, queues):
            for h in range(HALVES):
                queues[h].dma_start(
                    out=out[P * h:P * (h + 1), slots(m, e, count)], in_=results[m, h][:, SLOTS * e:SLOTS * (e + count)]
                )

        for i in range(len(CHUNKS)):
            interleave(i)

        quantize(0)
        quantize(1)
        for e in range(E):
            gather_words(0, 0, e)
        quantize(2)
        for e in range(E):
            gather_scales(0, e)
        shift(slots(0, 0, E), g_scales[:, slots(0, 0, E)])
        for e in range(E):
            gather_words(0, 1, e)
        quantize(3)
        for j, e in enumerate((2, 3)):
            gather(1, e, scales, g_early[:, SLOTS * j:SLOTS * (j + 1)])
        shift(slots(1, 2, 2), g_early[:])
        gather_words(1, 0, 2)
        quantize(4, 0)
        quantize(4, 1)
        gather_scales(1, 0)
        gather_scales(1, 1)
        shift(slots(1, 0, 2), g_scales[:, slots(1, 0, 2)])
        gather_scales(1, 2)
        gather_words(1, 1, 2)
        gather_words(1, 0, 3)
        gather_scales(1, 3)
        gather_words(1, 1, 3)
        gather_words(1, 0, 0)
        gather_words(1, 0, 1)
        gather_words(1, 1, 0)
        gather_words(1, 1, 1)

        for e in range(E):
            multiply(0, e)
        for e in range(E):
            activate(0, e)
            if e % 2 == 1:
                store(0, e - 1, 2, (nc.scalar, nc.scalar))
        for e in (2, 3, 0, 1):
            multiply(1, e)
            activate(1, e)
            if e == 3:
                store(1, 2, 2, (nc.sync, nc.sync))
            if e < 2:
                store(1, e, 1, (nc.sync, nc.scalar))
